import numpy as np
import ml_dtypes


def mxq(x, axis, fmt="e4m3"):
    dtype, down = {"e4m3": (ml_dtypes.float8_e4m3fn, 7), "e5m2": (ml_dtypes.float8_e5m2, 14)}[fmt]
    v = np.moveaxis(np.asarray(x, np.float32).astype(ml_dtypes.bfloat16).astype(np.float64), axis, -1)
    blocks = v.reshape(v.shape[:-1] + (-1, 32))
    amax = np.abs(blocks).max(-1, keepdims=True)
    byte = np.maximum(np.where(amax > 0, np.frexp(amax)[1] - 1 + 127, 0) - down, 1)
    scale = np.exp2(byte - 127.0)
    codes = (blocks / scale).astype(np.float32).astype(dtype).astype(np.float64)
    return np.moveaxis((codes * scale).reshape(v.shape), -1, axis)


WIDE = False


def mx_kscale(k):
    if not WIDE:
        return np.ones(k)
    levels = np.array([10, -10, 5, -5, 0])
    if k % 512:
        return np.exp2(np.random.permutation(np.resize(levels, k // 32))).repeat(32)
    a = np.empty((k // 512, 16))
    for p in range(k // 512):
        a[p, :8] = np.random.permutation(np.resize(levels, 8))
        for g in range(8):
            far = levels[np.abs(levels - a[p, g]) >= 10]
            a[p, g + 8] = far[np.random.randint(len(far))]
    return np.exp2(a.ravel()).repeat(32)


def f64(x):
    return np.asarray(x).astype(np.float64)


def striped(idx):
    return np.tile(idx.reshape(-1, 16).T, (8, 1)).astype(np.uint16)


def unstriped(offs):
    return offs[:16].T.reshape(-1).astype(np.int64)


def striped8(idx):
    return np.concatenate([x.reshape(-1, 16).T for x in idx]).astype(np.uint16)


def runs(offs, k):
    lists = np.stack([offs[16 * r : 16 * r + 16].T.reshape(-1) for r in range(8)]).astype(np.int64)
    return lists[np.arange(k) % 512 // 64]


def pack_weight(w):
    k, n = w.shape
    w = f64(np.asarray(w, np.float32).astype(ml_dtypes.bfloat16)).reshape(k // 32, 32, n)
    amax = np.abs(w).max(1)
    byte = np.clip(np.where(amax > 0, np.frexp(amax)[1] - 1 + 127 - 7, 1), 1, 254)
    scaled = (w * np.exp2(127.0 - byte)[:, None, :]).reshape(k, n).astype(np.float32)
    words = np.ascontiguousarray(scaled.reshape(k // 512, 128, 4, n).transpose(0, 1, 3, 2)).astype(ml_dtypes.float8_e4m3fn).view(np.uint8)
    return words, np.ascontiguousarray(byte.astype(np.uint8).reshape(k // 512, 16, n))


def unpack_weight(words, scales):
    g, p, n, _ = words.shape
    vals = np.ascontiguousarray(words).view(ml_dtypes.float8_e4m3fn).astype(np.float64) * np.repeat(np.exp2(scales.astype(np.float64) - 127.0), 8, axis=1)[..., None]
    return vals.transpose(0, 1, 3, 2).reshape(g * 512, n)


def sigmoid(v):
    return 1.0 / (1.0 + np.exp(-np.maximum(v, -700.0)))


K, T, S, N = 512, 2048, 512, 128


def setup_inputs():
    n = np.random.standard_normal
    s = mx_kscale(K)[:, None]
    packed_xT = pack_weight(n((K, T)) * s)
    return {
        "x_words": packed_xT[0],
        "x_scales": packed_xT[1],
        "w1": (n((K, N)) / np.sqrt(K) / s).astype(np.float32),
        "w2": (n((K, N)) / np.sqrt(K) / s).astype(np.float32),
        "offs": striped8(np.stack([np.random.permutation(T)[:S] for _ in range(8)])),
        "own": striped(np.random.permutation(T)[:S]),
    }


def reference(x_words, x_scales, w1, w2, offs, own):
    xq = unpack_weight(x_words, x_scales)[np.arange(K)[:, None], runs(offs, K)]
    y = mxq(f64(w1), 0, "e4m3").T @ xq
    xown = unpack_weight(x_words, x_scales)[:, unstriped(own)]
    e = mxq(f64(w2), 0, "e4m3").T @ xown
    return sigmoid(y) * e

@@ -1,0 +1,104 @@
+from contextlib import ExitStack
+
+import concourse.mybir as mybir
+
+F32 = mybir.dt.float32
+BF16 = mybir.dt.bfloat16
+I32 = mybir.dt.int32
+U32 = mybir.dt.uint32
+U16 = mybir.dt.uint16
+U8 = mybir.dt.uint8
+FP8X4 = mybir.dt.float8_e4m3fn_x4
+SIGMOID = mybir.ActivationFunctionType.Sigmoid
+MULT = mybir.AluOpType.mult
+
+P = 128
+PACK = 4
+K, T, S, M = 512, 2048, 512, 128
+HALF = S // 2
+LIST_HALF = HALF // 16
+FLOPS = 2 * 2 * K * M * S
+
+
+def tile_picked_phmix_sigmoid_p_kernel(tc, x_words, x_scales, w1, w2, offs, own, out):
+    nc = tc.nc
+    with ExitStack() as ctx:
+        keep = ctx.enter_context(tc.tile_pool(name="keep", bufs=1))
+        psum = ctx.enter_context(tc.psum_pool(name="psum", bufs=1))
+
+        offs_sb = keep.tile([P, S // 16], U16, name="offs_sb")
+        own_sb = keep.tile([P, S // 16], U16, name="own_sb")
+        nc.sync.dma_start(offs_sb[:], offs)
+        nc.sync.dma_start(own_sb[:], own)
+
+        scale_table = keep.tile([P, T], U8, name="scale_table", tag="slot_a", align_bytes=64)
+        nc.vector.memset(scale_table[:].bitcast(I32), 0)
+        nc.scalar.dma_start(scale_table[0:P:8, :].bitcast(I32), x_scales[0].bitcast(I32))
+
+        warm = keep.tile([P, 2], F32, name="warm")
+        nc.vector.memset(warm[:, 0:1], 0.0)
+        nc.scalar.activation(warm[:, 1:2], warm[:, 0:1], SIGMOID)
+
+        word_table = keep.tile([P, T], I32, name="word_table", align_bytes=64)
+        nc.sync.dma_start(word_table[:], x_words[0].rearrange("p c r -> p (c r)").bitcast(I32))
+
+        raws = []
+        for n, w in enumerate((w1, w2)):
+            raw = keep.tile([P, PACK, M], F32, name="raw%d" % n)
+            nc.sync.dma_start(raw[:], w.rearrange("(p j) m -> p j m", j=PACK))
+            raws.append(raw)
+
+        x_plane = keep.tile([P, 2 * S], U8, name="x_plane", align_bytes=64)
+        nc.vector.memset(x_plane[:].bitcast(I32), 0)
+
+        picked_scales = keep.tile([P, 2 * S], U8, name="picked_scales", align_bytes=64)
+        nc.vector.tensor_copy(picked_scales[:, 0:S], scale_table[:].indirect(offs_sb[:]))
+        nc.vector.tensor_copy(picked_scales[:, S : 2 * S], scale_table[:].indirect(own_sb[:]))
+        for i in range(4):
+            nc.sync.dma_start(x_plane[i:P:32, :].bitcast(I32), picked_scales[8 * i : P : 32, :].bitcast(I32))
+
+        window = word_table[:].bitcast(U32)
+        y_words = keep.tile([P, S], U32, name="y_words", tag="slot_a", align_bytes=64)
+        nc.vector.tensor_copy(y_words[:], window.indirect(offs_sb[:]))
+
+        w_codes = []
+        w_scales = []
+        e_words = []
+        for n in range(2):
+            grouped = keep.tile([P, M, PACK], BF16, name="grouped%d" % n, tag="slot_w%d" % n, align_bytes=64)
+            nc.scalar.copy(
+                grouped[:].rearrange("p (c i) t -> p c t i", i=4),
+                raws[n][:].rearrange("p t (c i) -> p c t i", i=4),
+            )
+            codes = keep.tile([P, M], U32, name="w_codes%d" % n, align_bytes=64)
+            scales = keep.tile([P, M], U8, name="w_scales%d" % n, align_bytes=64)
+            nc.vector.quantize_mx(codes[:].bitcast(FP8X4), scales[:], grouped[:].rearrange("p m t -> p (m t)"))
+            w_codes.append(codes)
+            w_scales.append(scales)
+            words = keep.tile([P, HALF], U32, name="e_words%d" % n, tag="slot_w%d" % n, align_bytes=64)
+            nc.vector.tensor_copy(words[:], window.indirect(own_sb[:, n * LIST_HALF : (n + 1) * LIST_HALF]))
+            e_words.append(words)
+
+        gates = []
+        for h in range(2):
+            cols = slice(h * HALF, (h + 1) * HALF)
+            y = psum.tile([P, HALF], F32, name="y%d" % h)
+            nc.tensor.matmul_mx(
+                y[:], lhsT=w_codes[0][:].bitcast(FP8X4), lhsT_scale=w_scales[0][:],
+                rhs=y_words[:, cols].bitcast(FP8X4), rhs_scale=x_plane[:, cols], start=True, stop=True,
+            )
+            gate = keep.tile([P, HALF], F32, name="gate%d" % h)
+            nc.scalar.activation(gate[:], y[:], SIGMOID)
+            gates.append(gate)
+        for h in range(2):
+            cols = slice(h * HALF, (h + 1) * HALF)
+            e = psum.tile([P, HALF], F32, name="e%d" % h)
+            nc.tensor.matmul_mx(
+                e[:], lhsT=w_codes[1][:].bitcast(FP8X4), lhsT_scale=w_scales[1][:],
+                rhs=e_words[h][:].bitcast(FP8X4), rhs_scale=x_plane[:, S + h * HALF : S + (h + 1) * HALF],
+                start=True, stop=True,
+            )
+            result = keep.tile([P, HALF], F32, name="result%d" % h)
+            nc.vector.tensor_tensor(result[:], e[:], gates[h][:], MULT)
+            queue = nc.sync if h == 0 else nc.scalar
+            queue.dma_start(out[:, cols], result[:])

@@ -29,11 +29,12 @@ def tile_picked_phmix_sigmoid_p_kernel(tc, x_words, x_scales, w1, w2, offs, own,
         offs_sb = keep.tile([P, S // 16], U16, name="offs_sb")
         own_sb = keep.tile([P, S // 16], U16, name="own_sb")
         nc.sync.dma_start(offs_sb[:], offs)
+        scale_table = keep.tile([P, T], U8, name="scale_table", align_bytes=64)
+        nc.sync.dma_start(
+            scale_table[:].bitcast(I32),
+            x_scales[0].bitcast(I32).unsqueeze(1).to_broadcast([16, 8, T // 4]),
+        )
         nc.sync.dma_start(own_sb[:], own)
-
-        scale_table = keep.tile([P, T], U8, name="scale_table", tag="slot_a", align_bytes=64)
-        nc.vector.memset(scale_table[:].bitcast(I32), 0)
-        nc.scalar.dma_start(scale_table[0:P:8, :].bitcast(I32), x_scales[0].bitcast(I32))
 
         warm = keep.tile([P, 2], F32, name="warm")
         nc.vector.memset(warm[:, 0:1], 0.0)
@@ -48,17 +49,19 @@ def tile_picked_phmix_sigmoid_p_kernel(tc, x_words, x_scales, w1, w2, offs, own,
             nc.sync.dma_start(raw[:], w.rearrange("(p j) m -> p j m", j=PACK))
             raws.append(raw)
 
-        x_plane = keep.tile([P, 2 * S], U8, name="x_plane", align_bytes=64)
-        nc.vector.memset(x_plane[:].bitcast(I32), 0)
-
-        picked_scales = keep.tile([P, 2 * S], U8, name="picked_scales", align_bytes=64)
-        nc.vector.tensor_copy(picked_scales[:, 0:S], scale_table[:].indirect(offs_sb[:]))
-        nc.vector.tensor_copy(picked_scales[:, S : 2 * S], scale_table[:].indirect(own_sb[:]))
-        for i in range(4):
-            nc.sync.dma_start(x_plane[i:P:32, :].bitcast(I32), picked_scales[8 * i : P : 32, :].bitcast(I32))
+        planes = []
+        for n, index in enumerate((offs_sb, own_sb)):
+            plane = keep.tile([P, S], U8, name="plane%d" % n, align_bytes=64)
+            nc.vector.memset(plane[:].bitcast(I32), 0)
+            picked = keep.tile([P, S], U8, name="picked%d" % n, align_bytes=64)
+            nc.vector.tensor_copy(picked[:], scale_table[:].indirect(index[:]))
+            for i in range(4):
+                queue = nc.scalar if n == 0 else nc.sync
+                queue.dma_start(plane[i:P:32, :].bitcast(I32), picked[8 * i : P : 32, :].bitcast(I32))
+            planes.append(plane)
 
         window = word_table[:].bitcast(U32)
-        y_words = keep.tile([P, S], U32, name="y_words", tag="slot_a", align_bytes=64)
+        y_words = keep.tile([P, S], U32, name="y_words", align_bytes=64)
         nc.vector.tensor_copy(y_words[:], window.indirect(offs_sb[:]))
 
         w_codes = []
@@ -85,7 +88,7 @@ def tile_picked_phmix_sigmoid_p_kernel(tc, x_words, x_scales, w1, w2, offs, own,
             y = psum.tile([P, HALF], F32, name="y%d" % h)
             nc.tensor.matmul_mx(
                 y[:], lhsT=w_codes[0][:].bitcast(FP8X4), lhsT_scale=w_scales[0][:],
-                rhs=y_words[:, cols].bitcast(FP8X4), rhs_scale=x_plane[:, cols], start=True, stop=True,
+                rhs=y_words[:, cols].bitcast(FP8X4), rhs_scale=planes[0][:, cols], start=True, stop=True,
             )
             gate = keep.tile([P, HALF], F32, name="gate%d" % h)
             nc.scalar.activation(gate[:], y[:], SIGMOID)
@@ -95,7 +98,7 @@ def tile_picked_phmix_sigmoid_p_kernel(tc, x_words, x_scales, w1, w2, offs, own,
             e = psum.tile([P, HALF], F32, name="e%d" % h)
             nc.tensor.matmul_mx(
                 e[:], lhsT=w_codes[1][:].bitcast(FP8X4), lhsT_scale=w_scales[1][:],
-                rhs=e_words[h][:].bitcast(FP8X4), rhs_scale=x_plane[:, S + h * HALF : S + (h + 1) * HALF],
+                rhs=e_words[h][:].bitcast(FP8X4), rhs_scale=planes[1][:, cols],
                 start=True, stop=True,
             )
             result = keep.tile([P, HALF], F32, name="result%d" % h)

@@ -16,6 +16,7 @@ P = 128
 PACK = 4
 K, T, S, M = 512, 2048, 512, 128
 HALF = S // 2
+QUARTER = S // 4
 LIST_HALF = HALF // 16
 FLOPS = 2 * 2 * K * M * S
 
@@ -29,12 +30,10 @@ def tile_picked_phmix_sigmoid_p_kernel(tc, x_words, x_scales, w1, w2, offs, own,
         offs_sb = keep.tile([P, S // 16], U16, name="offs_sb")
         own_sb = keep.tile([P, S // 16], U16, name="own_sb")
         nc.sync.dma_start(offs_sb[:], offs)
-        scale_table = keep.tile([P, T], U8, name="scale_table", align_bytes=64)
-        nc.sync.dma_start(
-            scale_table[:].bitcast(I32),
-            x_scales[0].bitcast(I32).unsqueeze(1).to_broadcast([16, 8, T // 4]),
-        )
         nc.sync.dma_start(own_sb[:], own)
+        scale_table = keep.tile([P, T], U8, name="scale_table", align_bytes=64)
+        nc.vector.memset(scale_table[:].bitcast(I32), 0)
+        nc.sync.dma_start(scale_table[0:P:8, :].bitcast(I32), x_scales[0].bitcast(I32))
 
         warm = keep.tile([P, 2], F32, name="warm")
         nc.vector.memset(warm[:, 0:1], 0.0)
@@ -45,7 +44,7 @@ def tile_picked_phmix_sigmoid_p_kernel(tc, x_words, x_scales, w1, w2, offs, own,
 
         raws = []
         for n, w in enumerate((w1, w2)):
-            raw = keep.tile([P, PACK, M], F32, name="raw%d" % n)
+            raw = keep.tile([P, PACK, M], F32, name="raw%d" % n, tag="slot_w%d" % n, align_bytes=64)
             nc.sync.dma_start(raw[:], w.rearrange("(p j) m -> p j m", j=PACK))
             raws.append(raw)
 
@@ -56,8 +55,7 @@ def tile_picked_phmix_sigmoid_p_kernel(tc, x_words, x_scales, w1, w2, offs, own,
             picked = keep.tile([P, S], U8, name="picked%d" % n, align_bytes=64)
             nc.vector.tensor_copy(picked[:], scale_table[:].indirect(index[:]))
             for i in range(4):
-                queue = nc.scalar if n == 0 else nc.sync
-                queue.dma_start(plane[i:P:32, :].bitcast(I32), picked[8 * i : P : 32, :].bitcast(I32))
+                nc.sync.dma_start(plane[i:P:32, :].bitcast(I32), picked[8 * i : P : 32, :].bitcast(I32))
             planes.append(plane)
 
         window = word_table[:].bitcast(U32)
@@ -68,7 +66,7 @@ def tile_picked_phmix_sigmoid_p_kernel(tc, x_words, x_scales, w1, w2, offs, own,
         w_scales = []
         e_words = []
         for n in range(2):
-            grouped = keep.tile([P, M, PACK], BF16, name="grouped%d" % n, tag="slot_w%d" % n, align_bytes=64)
+            grouped = keep.tile([P, M, PACK], BF16, name="grouped%d" % n, align_bytes=64)
             nc.scalar.copy(
                 grouped[:].rearrange("p (c i) t -> p c t i", i=4),
                 raws[n][:].rearrange("p t (c i) -> p c t i", i=4),
@@ -93,15 +91,20 @@ def tile_picked_phmix_sigmoid_p_kernel(tc, x_words, x_scales, w1, w2, offs, own,
             gate = keep.tile([P, HALF], F32, name="gate%d" % h)
             nc.scalar.activation(gate[:], y[:], SIGMOID)
             gates.append(gate)
-        for h in range(2):
-            cols = slice(h * HALF, (h + 1) * HALF)
-            e = psum.tile([P, HALF], F32, name="e%d" % h)
+        result = keep.tile([P, S], F32, name="result")
+        for g in range(4):
+            h, part = divmod(g, 2)
+            cols = slice(g * QUARTER, (g + 1) * QUARTER)
+            half_cols = slice(part * QUARTER, (part + 1) * QUARTER)
+            e = psum.tile([P, QUARTER], F32, name="e%d" % g)
             nc.tensor.matmul_mx(
                 e[:], lhsT=w_codes[1][:].bitcast(FP8X4), lhsT_scale=w_scales[1][:],
-                rhs=e_words[h][:].bitcast(FP8X4), rhs_scale=planes[1][:, cols],
+                rhs=e_words[h][:, half_cols].bitcast(FP8X4), rhs_scale=planes[1][:, cols],
                 start=True, stop=True,
             )
-            result = keep.tile([P, HALF], F32, name="result%d" % h)
-            nc.vector.tensor_tensor(result[:], e[:], gates[h][:], MULT)
-            queue = nc.sync if h == 0 else nc.scalar
-            queue.dma_start(out[:, cols], result[:])
+            nc.vector.tensor_tensor(result[:, cols], e[:], gates[h][:, half_cols], MULT)
+            if g == 1:
+                nc.sync.dma_start(out[:, 0:HALF], result[:, 0:HALF])
+            if g > 1:
+                queue = nc.scalar if g == 2 else nc.sync
+                queue.dma_start(out[:, cols], result[:, cols])

@@ -103,8 +103,6 @@ def tile_picked_phmix_sigmoid_p_kernel(tc, x_words, x_scales, w1, w2, offs, own,
                 start=True, stop=True,
             )
             nc.vector.tensor_tensor(result[:, cols], e[:], gates[h][:, half_cols], MULT)
-            if g == 1:
-                nc.sync.dma_start(out[:, 0:HALF], result[:, 0:HALF])
-            if g > 1:
-                queue = nc.scalar if g == 2 else nc.sync
-                queue.dma_start(out[:, cols], result[:, cols])
+            if part == 1:
+                stored = slice(h * HALF, (h + 1) * HALF)
+                nc.sync.dma_start(out[:, stored], result[:, stored])

@@ -51,10 +51,13 @@ def tile_picked_phmix_sigmoid_p_kernel(tc, x_words, x_scales, w1, w2, offs, own,
         planes = []
         for n, index in enumerate((offs_sb, own_sb)):
             plane = keep.tile([P, S], U8, name="plane%d" % n, align_bytes=64)
-            nc.vector.memset(plane[:].bitcast(I32), 0)
+            if n == 0:
+                nc.vector.memset(plane[:].bitcast(I32), 0)
             picked = keep.tile([P, S], U8, name="picked%d" % n, align_bytes=64)
             nc.vector.tensor_copy(picked[:], scale_table[:].indirect(index[:]))
-            for i in range(4):
+            if n == 1:
+                nc.vector.tensor_copy(plane[:].bitcast(I32), picked[:].bitcast(I32))
+            for i in range(n, 4):
                 nc.sync.dma_start(plane[i:P:32, :].bitcast(I32), picked[8 * i : P : 32, :].bitcast(I32))
             planes.append(plane)
 

@@ -18,6 +18,7 @@ K, T, S, M = 512, 2048, 512, 128
 HALF = S // 2
 QUARTER = S // 4
 LIST_HALF = HALF // 16
+ZEROED = T // 2
 FLOPS = 2 * 2 * K * M * S
 
 
@@ -29,11 +30,13 @@ def tile_picked_phmix_sigmoid_p_kernel(tc, x_words, x_scales, w1, w2, offs, own,
 
         offs_sb = keep.tile([P, S // 16], U16, name="offs_sb")
         own_sb = keep.tile([P, S // 16], U16, name="own_sb")
-        nc.sync.dma_start(offs_sb[:], offs)
-        nc.sync.dma_start(own_sb[:], own)
         scale_table = keep.tile([P, T], U8, name="scale_table", align_bytes=64)
-        nc.vector.memset(scale_table[:].bitcast(I32), 0)
-        nc.sync.dma_start(scale_table[0:P:8, :].bitcast(I32), x_scales[0].bitcast(I32))
+        spread = x_scales[0][:, ZEROED:T].bitcast(I32).unsqueeze(1).broadcast_to([16, 8, (T - ZEROED) // 4])
+        nc.sync.dma_start(scale_table[:, ZEROED:T].bitcast(I32), spread)
+        nc.sync.dma_start(offs_sb[:], offs)
+        nc.vector.memset(scale_table[:, 0:ZEROED].bitcast(I32), 0)
+        nc.sync.dma_start(scale_table[0:P:8, 0:ZEROED].bitcast(I32), x_scales[0][:, 0:ZEROED].bitcast(I32))
+        nc.sync.dma_start(own_sb[:], own)
 
         warm = keep.tile([P, 2], F32, name="warm")
         nc.vector.memset(warm[:, 0:1], 0.0)

@@ -51,18 +51,21 @@ def tile_picked_phmix_sigmoid_p_kernel(tc, x_words, x_scales, w1, w2, offs, own,
             nc.sync.dma_start(raw[:], w.rearrange("(p j) m -> p j m", j=PACK))
             raws.append(raw)
 
-        planes = []
-        for n, index in enumerate((offs_sb, own_sb)):
-            plane = keep.tile([P, S], U8, name="plane%d" % n, align_bytes=64)
-            if n == 0:
-                nc.vector.memset(plane[:].bitcast(I32), 0)
-            picked = keep.tile([P, S], U8, name="picked%d" % n, align_bytes=64)
-            nc.vector.tensor_copy(picked[:], scale_table[:].indirect(index[:]))
-            if n == 1:
-                nc.vector.tensor_copy(plane[:].bitcast(I32), picked[:].bitcast(I32))
-            for i in range(n, 4):
-                nc.sync.dma_start(plane[i:P:32, :].bitcast(I32), picked[8 * i : P : 32, :].bitcast(I32))
-            planes.append(plane)
+        early_plane = keep.tile([P, HALF], U8, name="early_plane", align_bytes=64)
+        late_plane = keep.tile([P, HALF + S], U8, name="late_plane", align_bytes=64)
+        nc.vector.memset(late_plane[:].bitcast(I32), 0)
+        early = keep.tile([P, HALF], U8, name="early", align_bytes=64)
+        late = keep.tile([P, HALF + S], U8, name="late", align_bytes=64)
+        nc.vector.tensor_copy(early[:], scale_table[:].indirect(offs_sb[:, 0:LIST_HALF]))
+        nc.vector.tensor_copy(late[:, 0:HALF], scale_table[:].indirect(offs_sb[:, LIST_HALF : 2 * LIST_HALF]))
+        nc.vector.tensor_copy(early_plane[:].bitcast(I32), early[:].bitcast(I32))
+        for i in range(1, 4):
+            nc.sync.dma_start(early_plane[i:P:32, :].bitcast(I32), early[8 * i : P : 32, :].bitcast(I32))
+        nc.vector.tensor_copy(late[:, HALF : HALF + S], scale_table[:].indirect(own_sb[:]))
+        for i in range(4):
+            nc.sync.dma_start(late_plane[i:P:32, :].bitcast(I32), late[8 * i : P : 32, :].bitcast(I32))
+        y_planes = [early_plane[:], late_plane[:, 0:HALF]]
+        e_plane = late_plane[:, HALF : HALF + S]
 
         window = word_table[:].bitcast(U32)
         y_words = keep.tile([P, S], U32, name="y_words", align_bytes=64)
@@ -92,7 +95,7 @@ def tile_picked_phmix_sigmoid_p_kernel(tc, x_words, x_scales, w1, w2, offs, own,
             y = psum.tile([P, HALF], F32, name="y%d" % h)
             nc.tensor.matmul_mx(
                 y[:], lhsT=w_codes[0][:].bitcast(FP8X4), lhsT_scale=w_scales[0][:],
-                rhs=y_words[:, cols].bitcast(FP8X4), rhs_scale=planes[0][:, cols], start=True, stop=True,
+                rhs=y_words[:, cols].bitcast(FP8X4), rhs_scale=y_planes[h], start=True, stop=True,
             )
             gate = keep.tile([P, HALF], F32, name="gate%d" % h)
             nc.scalar.activation(gate[:], y[:], SIGMOID)
@@ -105,7 +108,7 @@ def tile_picked_phmix_sigmoid_p_kernel(tc, x_words, x_scales, w1, w2, offs, own,
             e = psum.tile([P, QUARTER], F32, name="e%d" % g)
             nc.tensor.matmul_mx(
                 e[:], lhsT=w_codes[1][:].bitcast(FP8X4), lhsT_scale=w_scales[1][:],
-                rhs=e_words[h][:, half_cols].bitcast(FP8X4), rhs_scale=planes[1][:, cols],
+                rhs=e_words[h][:, half_cols].bitcast(FP8X4), rhs_scale=e_plane[:, cols],
                 start=True, stop=True,
             )
             nc.vector.tensor_tensor(result[:, cols], e[:], gates[h][:, half_cols], MULT)

@@ -9,16 +9,25 @@ U32 = mybir.dt.uint32
 U16 = mybir.dt.uint16
 U8 = mybir.dt.uint8
 FP8X4 = mybir.dt.float8_e4m3fn_x4
-SIGMOID = mybir.ActivationFunctionType.Sigmoid
+COPY = mybir.ActivationFunctionType.Copy
+TANH = mybir.ActivationFunctionType.Tanh
 MULT = mybir.AluOpType.mult
+ADD = mybir.AluOpType.add
 
 P = 128
 PACK = 4
 K, T, S, M = 512, 2048, 512, 128
+BLOCKS = K // 32
+BLOCK_PARTS = P // BLOCKS
+QUADRANT = 32
+PLANE_ROWS = 4
+GROUP = 16
 HALF = S // 2
 QUARTER = S // 4
-LIST_HALF = HALF // 16
-ZEROED = T // 2
+LIST_HALF = HALF // GROUP
+HALF_ROW = T // 2
+CAST_SCALES = (1.0, 0.5)
+CAST_RUN = 4
 FLOPS = 2 * 2 * K * M * S
 
 
@@ -28,19 +37,18 @@ def tile_picked_phmix_sigmoid_p_kernel(tc, x_words, x_scales, w1, w2, offs, own,
         keep = ctx.enter_context(tc.tile_pool(name="keep", bufs=1))
         psum = ctx.enter_context(tc.psum_pool(name="psum", bufs=1))
 
-        offs_sb = keep.tile([P, S // 16], U16, name="offs_sb")
-        own_sb = keep.tile([P, S // 16], U16, name="own_sb")
+        offs_sb = keep.tile([P, S // GROUP], U16, name="offs_sb")
+        own_sb = keep.tile([P, S // GROUP], U16, name="own_sb")
         scale_table = keep.tile([P, T], U8, name="scale_table", align_bytes=64)
-        spread = x_scales[0][:, ZEROED:T].bitcast(I32).unsqueeze(1).broadcast_to([16, 8, (T - ZEROED) // 4])
-        nc.sync.dma_start(scale_table[:, ZEROED:T].bitcast(I32), spread)
+        half_rows = x_scales[0].rearrange("b (h c) -> (b h) c", h=2).bitcast(I32)
+        repeated = half_rows.unsqueeze(1).broadcast_to([2 * BLOCKS, BLOCK_PARTS // 2, HALF_ROW // PACK])
+        nc.sync.dma_start(scale_table[:, 0:HALF_ROW].bitcast(I32), repeated)
         nc.sync.dma_start(offs_sb[:], offs)
-        nc.vector.memset(scale_table[:, 0:ZEROED].bitcast(I32), 0)
-        nc.sync.dma_start(scale_table[0:P:8, 0:ZEROED].bitcast(I32), x_scales[0][:, 0:ZEROED].bitcast(I32))
+        nc.vector.memset(scale_table[:, HALF_ROW:T].bitcast(I32), 0)
+        nc.sync.dma_start(
+            scale_table[0:P:BLOCK_PARTS, HALF_ROW:T].bitcast(I32), x_scales[0][:, HALF_ROW:T].bitcast(I32)
+        )
         nc.sync.dma_start(own_sb[:], own)
-
-        warm = keep.tile([P, 2], F32, name="warm")
-        nc.vector.memset(warm[:, 0:1], 0.0)
-        nc.scalar.activation(warm[:, 1:2], warm[:, 0:1], SIGMOID)
 
         word_table = keep.tile([P, T], I32, name="word_table", align_bytes=64)
         nc.sync.dma_start(word_table[:], x_words[0].rearrange("p c r -> p (c r)").bitcast(I32))
@@ -59,11 +67,15 @@ def tile_picked_phmix_sigmoid_p_kernel(tc, x_words, x_scales, w1, w2, offs, own,
         nc.vector.tensor_copy(early[:], scale_table[:].indirect(offs_sb[:, 0:LIST_HALF]))
         nc.vector.tensor_copy(late[:, 0:HALF], scale_table[:].indirect(offs_sb[:, LIST_HALF : 2 * LIST_HALF]))
         nc.vector.tensor_copy(early_plane[:].bitcast(I32), early[:].bitcast(I32))
-        for i in range(1, 4):
-            nc.sync.dma_start(early_plane[i:P:32, :].bitcast(I32), early[8 * i : P : 32, :].bitcast(I32))
+        for i in range(1, PLANE_ROWS):
+            nc.sync.dma_start(
+                early_plane[i:P:QUADRANT, :].bitcast(I32), early[BLOCK_PARTS * i : P : QUADRANT, :].bitcast(I32)
+            )
         nc.vector.tensor_copy(late[:, HALF : HALF + S], scale_table[:].indirect(own_sb[:]))
-        for i in range(4):
-            nc.sync.dma_start(late_plane[i:P:32, :].bitcast(I32), late[8 * i : P : 32, :].bitcast(I32))
+        for i in range(PLANE_ROWS):
+            nc.sync.dma_start(
+                late_plane[i:P:QUADRANT, :].bitcast(I32), late[BLOCK_PARTS * i : P : QUADRANT, :].bitcast(I32)
+            )
         y_planes = [early_plane[:], late_plane[:, 0:HALF]]
         e_plane = late_plane[:, HALF : HALF + S]
 
@@ -76,9 +88,10 @@ def tile_picked_phmix_sigmoid_p_kernel(tc, x_words, x_scales, w1, w2, offs, own,
         e_words = []
         for n in range(2):
             grouped = keep.tile([P, M, PACK], BF16, name="grouped%d" % n, align_bytes=64)
-            nc.scalar.copy(
-                grouped[:].rearrange("p (c i) t -> p c t i", i=4),
-                raws[n][:].rearrange("p t (c i) -> p c t i", i=4),
+            nc.scalar.activation(
+                grouped[:].rearrange("p (c i) t -> p c t i", i=CAST_RUN),
+                raws[n][:].rearrange("p t (c i) -> p c t i", i=CAST_RUN),
+                COPY, scale=CAST_SCALES[n],
             )
             codes = keep.tile([P, M], U32, name="w_codes%d" % n, align_bytes=64)
             scales = keep.tile([P, M], U8, name="w_scales%d" % n, align_bytes=64)
@@ -89,7 +102,7 @@ def tile_picked_phmix_sigmoid_p_kernel(tc, x_words, x_scales, w1, w2, offs, own,
             nc.vector.tensor_copy(words[:], window.indirect(own_sb[:, n * LIST_HALF : (n + 1) * LIST_HALF]))
             e_words.append(words)
 
-        gates = []
+        tanhs = []
         for h in range(2):
             cols = slice(h * HALF, (h + 1) * HALF)
             y = psum.tile([P, HALF], F32, name="y%d" % h)
@@ -97,21 +110,22 @@ def tile_picked_phmix_sigmoid_p_kernel(tc, x_words, x_scales, w1, w2, offs, own,
                 y[:], lhsT=w_codes[0][:].bitcast(FP8X4), lhsT_scale=w_scales[0][:],
                 rhs=y_words[:, cols].bitcast(FP8X4), rhs_scale=y_planes[h], start=True, stop=True,
             )
-            gate = keep.tile([P, HALF], F32, name="gate%d" % h)
-            nc.scalar.activation(gate[:], y[:], SIGMOID)
-            gates.append(gate)
+            tanh_half = keep.tile([P, HALF], F32, name="tanh%d" % h)
+            nc.scalar.activation(tanh_half[:], y[:], TANH, scale=0.5)
+            tanhs.append(tanh_half)
+
         result = keep.tile([P, S], F32, name="result")
-        for g in range(4):
+        for g in range(S // QUARTER):
             h, part = divmod(g, 2)
             cols = slice(g * QUARTER, (g + 1) * QUARTER)
             half_cols = slice(part * QUARTER, (part + 1) * QUARTER)
-            e = psum.tile([P, QUARTER], F32, name="e%d" % g)
+            e_halved = psum.tile([P, QUARTER], F32, name="e%d" % g)
             nc.tensor.matmul_mx(
-                e[:], lhsT=w_codes[1][:].bitcast(FP8X4), lhsT_scale=w_scales[1][:],
+                e_halved[:], lhsT=w_codes[1][:].bitcast(FP8X4), lhsT_scale=w_scales[1][:],
                 rhs=e_words[h][:, half_cols].bitcast(FP8X4), rhs_scale=e_plane[:, cols],
                 start=True, stop=True,
             )
-            nc.vector.tensor_tensor(result[:, cols], e[:], gates[h][:, half_cols], MULT)
+            nc.vector.scalar_tensor_tensor(result[:, cols], tanhs[h][:, half_cols], 1.0, e_halved[:], ADD, MULT)
             if part == 1:
                 stored = slice(h * HALF, (h + 1) * HALF)
                 nc.sync.dma_start(out[:, stored], result[:, stored])

@@ -16,6 +16,7 @@ ADD = mybir.AluOpType.add
 
 P = 128
 PACK = 4
+I32_BYTES = 4
 K, T, S, M = 512, 2048, 512, 128
 BLOCKS = K // 32
 BLOCK_PARTS = P // BLOCKS
@@ -26,7 +27,6 @@ HALF = S // 2
 QUARTER = S // 4
 LIST_HALF = HALF // GROUP
 HALF_ROW = T // 2
-CAST_SCALES = (1.0, 0.5)
 CAST_RUN = 4
 FLOPS = 2 * 2 * K * M * S
 
@@ -41,7 +41,7 @@ def tile_picked_phmix_sigmoid_p_kernel(tc, x_words, x_scales, w1, w2, offs, own,
         own_sb = keep.tile([P, S // GROUP], U16, name="own_sb")
         scale_table = keep.tile([P, T], U8, name="scale_table", align_bytes=64)
         half_rows = x_scales[0].rearrange("b (h c) -> (b h) c", h=2).bitcast(I32)
-        repeated = half_rows.unsqueeze(1).broadcast_to([2 * BLOCKS, BLOCK_PARTS // 2, HALF_ROW // PACK])
+        repeated = half_rows.unsqueeze(1).broadcast_to([2 * BLOCKS, BLOCK_PARTS // 2, HALF_ROW // I32_BYTES])
         nc.sync.dma_start(scale_table[:, 0:HALF_ROW].bitcast(I32), repeated)
         nc.sync.dma_start(offs_sb[:], offs)
         nc.vector.memset(scale_table[:, HALF_ROW:T].bitcast(I32), 0)
@@ -88,11 +88,12 @@ def tile_picked_phmix_sigmoid_p_kernel(tc, x_words, x_scales, w1, w2, offs, own,
         e_words = []
         for n in range(2):
             grouped = keep.tile([P, M, PACK], BF16, name="grouped%d" % n, align_bytes=64)
-            nc.scalar.activation(
-                grouped[:].rearrange("p (c i) t -> p c t i", i=CAST_RUN),
-                raws[n][:].rearrange("p t (c i) -> p c t i", i=CAST_RUN),
-                COPY, scale=CAST_SCALES[n],
-            )
+            cast_out = grouped[:].rearrange("p (c i) t -> p c t i", i=CAST_RUN)
+            cast_in = raws[n][:].rearrange("p t (c i) -> p c t i", i=CAST_RUN)
+            if n == 0:
+                nc.scalar.copy(cast_out, cast_in)
+            else:
+                nc.scalar.activation(cast_out, cast_in, COPY, scale=0.5)
             codes = keep.tile([P, M], U32, name="w_codes%d" % n, align_bytes=64)
             scales = keep.tile([P, M], U8, name="w_scales%d" % n, align_bytes=64)
             nc.vector.quantize_mx(codes[:].bitcast(FP8X4), scales[:], grouped[:].rearrange("p m t -> p (m t)"))

@@ -44,11 +44,11 @@ def tile_picked_phmix_sigmoid_p_kernel(tc, x_words, x_scales, w1, w2, offs, own,
         repeated = half_rows.unsqueeze(1).broadcast_to([2 * BLOCKS, BLOCK_PARTS // 2, HALF_ROW // I32_BYTES])
         nc.sync.dma_start(scale_table[:, 0:HALF_ROW].bitcast(I32), repeated)
         nc.sync.dma_start(offs_sb[:], offs)
+        nc.sync.dma_start(own_sb[:], own)
         nc.vector.memset(scale_table[:, HALF_ROW:T].bitcast(I32), 0)
         nc.sync.dma_start(
             scale_table[0:P:BLOCK_PARTS, HALF_ROW:T].bitcast(I32), x_scales[0][:, HALF_ROW:T].bitcast(I32)
         )
-        nc.sync.dma_start(own_sb[:], own)
 
         word_table = keep.tile([P, T], I32, name="word_table", align_bytes=64)
         nc.sync.dma_start(word_table[:], x_words[0].rearrange("p c r -> p (c r)").bitcast(I32))
@@ -65,13 +65,13 @@ def tile_picked_phmix_sigmoid_p_kernel(tc, x_words, x_scales, w1, w2, offs, own,
         early = keep.tile([P, HALF], U8, name="early", align_bytes=64)
         late = keep.tile([P, HALF + S], U8, name="late", align_bytes=64)
         nc.vector.tensor_copy(early[:], scale_table[:].indirect(offs_sb[:, 0:LIST_HALF]))
-        nc.vector.tensor_copy(late[:, 0:HALF], scale_table[:].indirect(offs_sb[:, LIST_HALF : 2 * LIST_HALF]))
+        nc.vector.tensor_copy(late[:, HALF : HALF + S], scale_table[:].indirect(own_sb[:]))
         nc.vector.tensor_copy(early_plane[:].bitcast(I32), early[:].bitcast(I32))
         for i in range(1, PLANE_ROWS):
             nc.sync.dma_start(
                 early_plane[i:P:QUADRANT, :].bitcast(I32), early[BLOCK_PARTS * i : P : QUADRANT, :].bitcast(I32)
             )
-        nc.vector.tensor_copy(late[:, HALF : HALF + S], scale_table[:].indirect(own_sb[:]))
+        nc.vector.tensor_copy(late[:, 0:HALF], scale_table[:].indirect(offs_sb[:, LIST_HALF : 2 * LIST_HALF]))
         for i in range(PLANE_ROWS):
             nc.sync.dma_start(
                 late_plane[i:P:QUADRANT, :].bitcast(I32), late[BLOCK_PARTS * i : P : QUADRANT, :].bitcast(I32)

from contextlib import ExitStack

import concourse.mybir as mybir

F32 = mybir.dt.float32
BF16 = mybir.dt.bfloat16
I32 = mybir.dt.int32
U32 = mybir.dt.uint32
U16 = mybir.dt.uint16
U8 = mybir.dt.uint8
FP8X4 = mybir.dt.float8_e4m3fn_x4
COPY = mybir.ActivationFunctionType.Copy
TANH = mybir.ActivationFunctionType.Tanh
MULT = mybir.AluOpType.mult
ADD = mybir.AluOpType.add

P = 128
PACK = 4
I32_BYTES = 4
K, T, S, M = 512, 2048, 512, 128
BLOCKS = K // 32
BLOCK_PARTS = P // BLOCKS
QUADRANT = 32
PLANE_ROWS = 4
GROUP = 16
HALF = S // 2
QUARTER = S // 4
LIST_HALF = HALF // GROUP
HALF_ROW = T // 2
CAST_RUN = 4
FLOPS = 2 * 2 * K * M * S


def tile_picked_phmix_sigmoid_p_kernel(tc, x_words, x_scales, w1, w2, offs, own, out):
    nc = tc.nc
    with ExitStack() as ctx:
        keep = ctx.enter_context(tc.tile_pool(name="keep", bufs=1))
        psum = ctx.enter_context(tc.psum_pool(name="psum", bufs=1))

        offs_sb = keep.tile([P, S // GROUP], U16, name="offs_sb")
        own_sb = keep.tile([P, S // GROUP], U16, name="own_sb")
        scale_table = keep.tile([P, T], U8, name="scale_table", align_bytes=64)
        half_rows = x_scales[0].rearrange("b (h c) -> (b h) c", h=2).bitcast(I32)
        repeated = half_rows.unsqueeze(1).broadcast_to([2 * BLOCKS, BLOCK_PARTS // 2, HALF_ROW // I32_BYTES])
        nc.sync.dma_start(scale_table[:, 0:HALF_ROW].bitcast(I32), repeated)
        nc.sync.dma_start(offs_sb[:], offs)
        nc.sync.dma_start(own_sb[:], own)
        nc.vector.memset(scale_table[:, HALF_ROW:T].bitcast(I32), 0)
        nc.sync.dma_start(
            scale_table[0:P:BLOCK_PARTS, HALF_ROW:T].bitcast(I32), x_scales[0][:, HALF_ROW:T].bitcast(I32)
        )

        word_table = keep.tile([P, T], I32, name="word_table", align_bytes=64)
        nc.sync.dma_start(word_table[:], x_words[0].rearrange("p c r -> p (c r)").bitcast(I32))

        raws = []
        for n, w in enumerate((w1, w2)):
            raw = keep.tile([P, PACK, M], F32, name="raw%d" % n, tag="slot_w%d" % n, align_bytes=64)
            nc.sync.dma_start(raw[:], w.rearrange("(p j) m -> p j m", j=PACK))
            raws.append(raw)

        early_plane = keep.tile([P, HALF], U8, name="early_plane", align_bytes=64)
        late_plane = keep.tile([P, HALF + S], U8, name="late_plane", align_bytes=64)
        nc.vector.memset(late_plane[:].bitcast(I32), 0)
        early = keep.tile([P, HALF], U8, name="early", align_bytes=64)
        late = keep.tile([P, HALF + S], U8, name="late", align_bytes=64)
        nc.vector.tensor_copy(early[:], scale_table[:].indirect(offs_sb[:, 0:LIST_HALF]))
        nc.vector.tensor_copy(late[:, HALF : HALF + S], scale_table[:].indirect(own_sb[:]))
        nc.vector.tensor_copy(early_plane[:].bitcast(I32), early[:].bitcast(I32))
        for i in range(1, PLANE_ROWS):
            nc.sync.dma_start(
                early_plane[i:P:QUADRANT, :].bitcast(I32), early[BLOCK_PARTS * i : P : QUADRANT, :].bitcast(I32)
            )
        nc.vector.tensor_copy(late[:, 0:HALF], scale_table[:].indirect(offs_sb[:, LIST_HALF : 2 * LIST_HALF]))
        for i in range(PLANE_ROWS):
            nc.sync.dma_start(
                late_plane[i:P:QUADRANT, :].bitcast(I32), late[BLOCK_PARTS * i : P : QUADRANT, :].bitcast(I32)
            )
        y_planes = [early_plane[:], late_plane[:, 0:HALF]]
        e_plane = late_plane[:, HALF : HALF + S]

        window = word_table[:].bitcast(U32)
        y_words = keep.tile([P, S], U32, name="y_words", align_bytes=64)
        nc.vector.tensor_copy(y_words[:], window.indirect(offs_sb[:]))

        w_codes = []
        w_scales = []
        e_words = []
        for n in range(2):
            grouped = keep.tile([P, M, PACK], BF16, name="grouped%d" % n, align_bytes=64)
            cast_out = grouped[:].rearrange("p (c i) t -> p c t i", i=CAST_RUN)
            cast_in = raws[n][:].rearrange("p t (c i) -> p c t i", i=CAST_RUN)
            if n == 0:
                nc.scalar.copy(cast_out, cast_in)
            else:
                nc.scalar.activation(cast_out, cast_in, COPY, scale=0.5)
            codes = keep.tile([P, M], U32, name="w_codes%d" % n, align_bytes=64)
            scales = keep.tile([P, M], U8, name="w_scales%d" % n, align_bytes=64)
            nc.vector.quantize_mx(codes[:].bitcast(FP8X4), scales[:], grouped[:].rearrange("p m t -> p (m t)"))
            w_codes.append(codes)
            w_scales.append(scales)
            words = keep.tile([P, HALF], U32, name="e_words%d" % n, tag="slot_w%d" % n, align_bytes=64)
            nc.vector.tensor_copy(words[:], window.indirect(own_sb[:, n * LIST_HALF : (n + 1) * LIST_HALF]))
            e_words.append(words)

        tanhs = []
        for h in range(2):
            cols = slice(h * HALF, (h + 1) * HALF)
            y = psum.tile([P, HALF], F32, name="y%d" % h)
            nc.tensor.matmul_mx(
                y[:], lhsT=w_codes[0][:].bitcast(FP8X4), lhsT_scale=w_scales[0][:],
                rhs=y_words[:, cols].bitcast(FP8X4), rhs_scale=y_planes[h], start=True, stop=True,
            )
            tanh_half = keep.tile([P, HALF], F32, name="tanh%d" % h)
            nc.scalar.activation(tanh_half[:], y[:], TANH, scale=0.5)
            tanhs.append(tanh_half)

        result = keep.tile([P, S], F32, name="result")
        for g in range(S // QUARTER):
            h, part = divmod(g, 2)
            cols = slice(g * QUARTER, (g + 1) * QUARTER)
            half_cols = slice(part * QUARTER, (part + 1) * QUARTER)
            e_halved = psum.tile([P, QUARTER], F32, name="e%d" % g)
            nc.tensor.matmul_mx(
                e_halved[:], lhsT=w_codes[1][:].bitcast(FP8X4), lhsT_scale=w_scales[1][:],
                rhs=e_words[h][:, half_cols].bitcast(FP8X4), rhs_scale=e_plane[:, cols],
                start=True, stop=True,
            )
            nc.vector.scalar_tensor_tensor(result[:, cols], tanhs[h][:, half_cols], 1.0, e_halved[:], ADD, MULT)
            if part == 1:
                stored = slice(h * HALF, (h + 1) * HALF)
                nc.sync.dma_start(out[:, stored], result[:, stored])
